import numpy as np
CORES = [0,1,16,17,32,33,48,49,64,65,80,81,96,97,112,113,136,137,152,153,168,169,184,185,200,201,216,217,232,233,248,249]
N = 32
def setup_inputs(rng):
    return {"x": rng.standard_normal((N, 128, 1024)).astype(np.float32)}
def reference(x):
    b = 1024 // N
    blocks = x.reshape(N, 128, N, b)
    return {"y": np.ascontiguousarray(blocks.transpose(2, 1, 0, 3)).reshape(N, 128, 1024)}

@@ -1,0 +1,73 @@
+from concourse.bass import DstId, RemoteDMATransfer
+
+B = 32
+SCRATCH = {
+    "stage": ("sbuf", [128, 1024], "float32"),
+    "land": ("sbuf", [128, 1024], "float32"),
+    "P": ("sbuf", [128, 2, 8, B], "float32"),
+    "Q": ("sbuf", [128, 8, 2, B], "float32"),
+}
+SEMAPHORES = ["local", "sent", "arrived"]
+
+
+def helper_dests(h, s):
+    seq = [16 * h + (2 * s + 2 + i) % 16 for i in range(14)]
+    near = 16 * (1 - h) + 8 * (s // 4)
+    far = 16 * (1 - h) + 8 * (1 - s // 4)
+    return {2: list(range(near, near + 8)), 6: list(range(far, far + 8)),
+            3: sorted(seq[:7]), 7: sorted(seq[7:])}
+
+
+def runs(ids):
+    out = []
+    for k, d in enumerate(ids):
+        if out and out[-1][1] + out[-1][2] == d:
+            out[-1][2] += 1
+        else:
+            out.append([k, d, 1])
+    return out
+
+
+def rank_program(g, core, T, topo):
+    h, chip, c = topo.host(core), topo.chip(core), core % 8
+    if chip % 2 != h:
+        return
+    s = chip // 2
+    base = core - c
+    table = helper_dests(h, s)
+
+    def to(dst, src_ap, dst_ap, eng):
+        rid, pid = topo.addr(dst, core)
+        return RemoteDMATransfer(dst_ids=[DstId(rid=rid, pnc=pid)], dma_engine_mask=1 << eng,
+                                 remote_sem=T.sem.arrived, src=src_ap, dst=dst_ap)
+
+    if c < 2:
+        r = T.rank_of(core)
+        g.dma_start(out=T.stage[:], in_=T.x[:]).then_inc(T.sem.local, 16)
+        g.dma_start(out=T.land[:, r * B:(r + 1) * B], in_=T.x[:, r * B:(r + 1) * B]).then_inc(T.sem.local, 16)
+        g.wait_ge(T.sem.local, 32)
+        sib = r ^ 1
+        by_size = {1: [(T.cores[sib], sib, T.land[:, r * B:(r + 1) * B])]}
+        for hc in sorted(table):
+            for k, d, n in runs(table[hc]):
+                by_size.setdefault(n, []).append((base + hc, d, T.P[:, c, k:k + n, :]))
+        total = 0
+        for n in sorted(by_size):
+            tr = [to(dst, T.stage[:, d * B:(d + n) * B], ap, e) for e, (dst, d, ap) in enumerate(by_size[n])]
+            g.remote_dma_fused(tr, local_sem=T.sem.sent)
+            total += len(tr)
+        g.wait_ge(T.sem.sent, total)
+        g.wait_ge(T.sem.arrived, 1 + 15)
+        g.dma_start(out=T.y[:], in_=T.land[:]).then_inc(T.sem.local, 16)
+        g.wait_ge(T.sem.local, 48)
+    elif c in table:
+        ids = table[c]
+        m = len(ids)
+        g.wait_ge(T.sem.arrived, 2 * len(runs(ids)))
+        for q in range(2):
+            g.dma_start(out=T.Q[:, 0:m, q, :], in_=T.P[:, q, 0:m, :]).then_inc(T.sem.local, 16)
+        g.wait_ge(T.sem.local, 32)
+        col = (8 * h + s) * 2 * B
+        tr = [to(T.cores[d], T.Q[:, k], T.land[:, col:col + 2 * B], k) for k, d in enumerate(ids)]
+        g.remote_dma_fused(tr, local_sem=T.sem.sent)
+        g.wait_ge(T.sem.sent, m)

@@ -4,66 +4,90 @@ B = 32
 SCRATCH = {
     "stage": ("sbuf", [128, 1024], "float32"),
     "land": ("sbuf", [128, 1024], "float32"),
-    "P": ("sbuf", [128, 2, 8, B], "float32"),
-    "Q": ("sbuf", [128, 8, 2, B], "float32"),
+    "P": ("sbuf", [128, 2, 5, B], "float32"),
+    "Q": ("sbuf", [128, 5, 2, B], "float32"),
 }
 SEMAPHORES = ["local", "sent", "arrived"]
 
 
-def helper_dests(h, s):
+def pieces(ids):
+    out, k = [], 0
+    while k < len(ids):
+        n = 1
+        while k + n < len(ids) and ids[k + n] == ids[k] + n:
+            n += 1
+        d = ids[k]
+        k += n
+        for z in (4, 2, 1):
+            while n >= z:
+                out.append((d, z))
+                d, n = d + z, n - z
+    return out
+
+
+def helpers(h, s):
     seq = [16 * h + (2 * s + 2 + i) % 16 for i in range(14)]
     near = 16 * (1 - h) + 8 * (s // 4)
-    far = 16 * (1 - h) + 8 * (1 - s // 4)
-    return {2: list(range(near, near + 8)), 6: list(range(far, far + 8)),
-            3: sorted(seq[:7]), 7: sorted(seq[7:])}
-
-
-def runs(ids):
-    out = []
-    for k, d in enumerate(ids):
-        if out and out[-1][1] + out[-1][2] == d:
-            out[-1][2] += 1
-        else:
-            out.append([k, d, 1])
-    return out
+    j = (s % 4) // 2
+    table = {2: [(near + 4 * j, 4)], 6: [(near + 4 * (1 - j), 4)], 3: pieces(seq[:5]), 4: [], 5: [], 7: []}
+    for p in sorted(pieces(seq[5:]), key=lambda p: -p[1]):
+        load, hc = min((sum(n for d, n in table[hc]), hc) for hc in (4, 5, 7))
+        table[hc].append(p)
+    return table
 
 
 def rank_program(g, core, T, topo):
     h, chip, c = topo.host(core), topo.chip(core), core % 8
-    if chip % 2 != h:
-        return
     s = chip // 2
-    base = core - c
-    table = helper_dests(h, s)
 
     def to(dst, src_ap, dst_ap, eng):
         rid, pid = topo.addr(dst, core)
         return RemoteDMATransfer(dst_ids=[DstId(rid=rid, pnc=pid)], dma_engine_mask=1 << eng,
                                  remote_sem=T.sem.arrived, src=src_ap, dst=dst_ap)
 
+    if chip % 2 != h:
+        if c not in (2, 6):
+            return
+        first = 16 * (1 - h) + 8 * (1 - s // 4) + (0 if c == 2 else 4)
+        g.wait_ge(T.sem.arrived, 4)
+        for t in range(2):
+            g.dma_start(out=T.P[:, t, 0:4, :], in_=T.Q[:, 0:4, t, :]).then_inc(T.sem.local, 16)
+        g.wait_ge(T.sem.local, 32)
+        tr = [to(T.cores[16 * h + 2 * s + t], T.P[:, t, 0:4, :], T.land[:, first * B:(first + 4) * B], t)
+              for t in range(2)]
+        g.remote_dma_fused(tr, local_sem=T.sem.sent)
+        g.wait_ge(T.sem.sent, 2)
+        return
+
+    table = helpers(h, s)
     if c < 2:
         r = T.rank_of(core)
         g.dma_start(out=T.stage[:], in_=T.x[:]).then_inc(T.sem.local, 16)
         g.dma_start(out=T.land[:, r * B:(r + 1) * B], in_=T.x[:, r * B:(r + 1) * B]).then_inc(T.sem.local, 16)
         g.wait_ge(T.sem.local, 32)
-        sib = r ^ 1
-        by_size = {1: [(T.cores[sib], sib, T.land[:, r * B:(r + 1) * B])]}
+        sends = {1: [], 2: [], 4: []}
+        for d in range(4 * (1 - s // 4), 4 * (1 - s // 4) + 4):
+            mate_helper = 128 * (1 - h) + 8 * (2 * d + h) + (2 if s % 4 < 2 else 6)
+            sends[2].append((mate_helper, 16 * (1 - h) + 2 * d, T.Q[:, 2 * (s % 2) + c]))
+        sends[1].append((T.cores[r ^ 1], r ^ 1, T.land[:, r * B:(r + 1) * B]))
         for hc in sorted(table):
-            for k, d, n in runs(table[hc]):
-                by_size.setdefault(n, []).append((base + hc, d, T.P[:, c, k:k + n, :]))
+            k = 0
+            for d, n in table[hc]:
+                sends[n].append((core - c + hc, d, T.P[:, c, k:k + n, :]))
+                k += n
         total = 0
-        for n in sorted(by_size):
-            tr = [to(dst, T.stage[:, d * B:(d + n) * B], ap, e) for e, (dst, d, ap) in enumerate(by_size[n])]
+        for n in sorted(sends):
+            tr = [to(dst, T.stage[:, d * B:(d + n) * B], ap, e) for e, (dst, d, ap) in enumerate(sends[n])]
             g.remote_dma_fused(tr, local_sem=T.sem.sent)
             total += len(tr)
         g.wait_ge(T.sem.sent, total)
-        g.wait_ge(T.sem.arrived, 1 + 15)
+        g.wait_ge(T.sem.arrived, 14)
         g.dma_start(out=T.y[:], in_=T.land[:]).then_inc(T.sem.local, 16)
         g.wait_ge(T.sem.local, 48)
-    elif c in table:
-        ids = table[c]
+    else:
+        ids = [d + i for d, n in table[c] for i in range(n)]
         m = len(ids)
-        g.wait_ge(T.sem.arrived, 2 * len(runs(ids)))
+        g.wait_ge(T.sem.arrived, 2 * len(table[c]))
         for q in range(2):
             g.dma_start(out=T.Q[:, 0:m, q, :], in_=T.P[:, q, 0:m, :]).then_inc(T.sem.local, 16)
         g.wait_ge(T.sem.local, 32)

from concourse.bass import DstId, RemoteDMATransfer

B = 32
SCRATCH = {
    "stage": ("sbuf", [128, 1024], "float32"),
    "land": ("sbuf", [128, 1024], "float32"),
    "P": ("sbuf", [128, 2, 5, B], "float32"),
    "Q": ("sbuf", [128, 5, 2, B], "float32"),
}
SEMAPHORES = ["local", "sent", "arrived"]


def pieces(ids):
    out, k = [], 0
    while k < len(ids):
        n = 1
        while k + n < len(ids) and ids[k + n] == ids[k] + n:
            n += 1
        d = ids[k]
        k += n
        for z in (4, 2, 1):
            while n >= z:
                out.append((d, z))
                d, n = d + z, n - z
    return out


def helpers(h, s):
    seq = [16 * h + (2 * s + 2 + i) % 16 for i in range(14)]
    near = 16 * (1 - h) + 8 * (s // 4)
    j = (s % 4) // 2
    table = {2: [(near + 4 * j, 4)], 6: [(near + 4 * (1 - j), 4)], 3: pieces(seq[:5]), 4: [], 5: [], 7: []}
    for p in sorted(pieces(seq[5:]), key=lambda p: -p[1]):
        load, hc = min((sum(n for d, n in table[hc]), hc) for hc in (4, 5, 7))
        table[hc].append(p)
    return table


def rank_program(g, core, T, topo):
    h, chip, c = topo.host(core), topo.chip(core), core % 8
    s = chip // 2

    def to(dst, src_ap, dst_ap, eng):
        rid, pid = topo.addr(dst, core)
        return RemoteDMATransfer(dst_ids=[DstId(rid=rid, pnc=pid)], dma_engine_mask=1 << eng,
                                 remote_sem=T.sem.arrived, src=src_ap, dst=dst_ap)

    if chip % 2 != h:
        if c not in (2, 6):
            return
        first = 16 * (1 - h) + 8 * (1 - s // 4) + (0 if c == 2 else 4)
        g.wait_ge(T.sem.arrived, 4)
        for t in range(2):
            g.dma_start(out=T.P[:, t, 0:4, :], in_=T.Q[:, 0:4, t, :]).then_inc(T.sem.local, 16)
        g.wait_ge(T.sem.local, 32)
        tr = [to(T.cores[16 * h + 2 * s + t], T.P[:, t, 0:4, :], T.land[:, first * B:(first + 4) * B], t)
              for t in range(2)]
        g.remote_dma_fused(tr, local_sem=T.sem.sent)
        g.wait_ge(T.sem.sent, 2)
        return

    table = helpers(h, s)
    if c < 2:
        r = T.rank_of(core)
        g.dma_start(out=T.stage[:], in_=T.x[:]).then_inc(T.sem.local, 16)
        g.dma_start(out=T.land[:, r * B:(r + 1) * B], in_=T.x[:, r * B:(r + 1) * B]).then_inc(T.sem.local, 16)
        g.wait_ge(T.sem.local, 32)
        sends = {1: [], 2: [], 4: []}
        for d in range(4 * (1 - s // 4), 4 * (1 - s // 4) + 4):
            mate_helper = 128 * (1 - h) + 8 * (2 * d + h) + (2 if s % 4 < 2 else 6)
            sends[2].append((mate_helper, 16 * (1 - h) + 2 * d, T.Q[:, 2 * (s % 2) + c]))
        sends[1].append((T.cores[r ^ 1], r ^ 1, T.land[:, r * B:(r + 1) * B]))
        for hc in sorted(table):
            k = 0
            for d, n in table[hc]:
                sends[n].append((core - c + hc, d, T.P[:, c, k:k + n, :]))
                k += n
        total = 0
        for n in sorted(sends):
            tr = [to(dst, T.stage[:, d * B:(d + n) * B], ap, e) for e, (dst, d, ap) in enumerate(sends[n])]
            g.remote_dma_fused(tr, local_sem=T.sem.sent)
            total += len(tr)
        g.wait_ge(T.sem.sent, total)
        g.wait_ge(T.sem.arrived, 14)
        g.dma_start(out=T.y[:], in_=T.land[:]).then_inc(T.sem.local, 16)
        g.wait_ge(T.sem.local, 48)
    else:
        ids = [d + i for d, n in table[c] for i in range(n)]
        m = len(ids)
        g.wait_ge(T.sem.arrived, 2 * len(table[c]))
        for q in range(2):
            g.dma_start(out=T.Q[:, 0:m, q, :], in_=T.P[:, q, 0:m, :]).then_inc(T.sem.local, 16)
        g.wait_ge(T.sem.local, 32)
        col = (8 * h + s) * 2 * B
        tr = [to(T.cores[d], T.Q[:, k], T.land[:, col:col + 2 * B], k) for k, d in enumerate(ids)]
        g.remote_dma_fused(tr, local_sem=T.sem.sent)
        g.wait_ge(T.sem.sent, m)
